import numpy as np
import ml_dtypes

BF16 = ml_dtypes.bfloat16


def bf(x):
    return np.asarray(x, np.float32).astype(BF16)


def f32(x):
    return np.asarray(x, np.float32)


def f64(x):
    return np.asarray(x).astype(np.float64)


def striped(idx):
    return np.tile(idx.reshape(-1, 16).T, (8, 1))


def rows(idx, k):
    return np.tile(idx, (k, 1))


def look(tab, idx):
    return np.take_along_axis(f64(tab), rows(idx, len(tab)), axis=1)


K, S, H, D, V, N = 128, 2048, 256, 2, 1024, 2048


def setup_inputs():
    return {"z": bf(np.random.standard_normal((H, S))), "wt": bf(np.random.standard_normal((H, K)) / np.sqrt(H)), "ctr": f32(1.0 * np.random.standard_normal((K, V))), "offs": striped(np.random.permutation(S)[:N])}


def reference(z, wt, ctr, offs):
    idx = offs[:16].T.reshape(-1)
    tab = f64(wt).T @ f64(z)
    x = sum(np.maximum(look(tab, idx[d * V:(d + 1) * V]) - f64(ctr), 0.0) for d in range(D))
    return x

@@ -1,0 +1,55 @@
+import concourse.mybir as mybir
+
+F32, BF16, U16 = mybir.dt.float32, mybir.dt.bfloat16, mybir.dt.uint16
+SUB, MAX, ADD = mybir.AluOpType.subtract, mybir.AluOpType.max, mybir.AluOpType.add
+RELU = mybir.ActivationFunctionType.Relu
+
+R, K, S, D, V = 128, 256, 2048, 2, 1024
+HALVES = K // 128
+BANK = 512
+PIECE = 512
+FLOPS = 2 * R * K * S + 3 * D * R * V
+
+
+def tile_lookup_pjedge_out_kernel(tc, z, wt, ctr, offs, out):
+    nc = tc.nc
+    with (
+        tc.tile_pool(name="lists", bufs=1) as lists,
+        tc.tile_pool(name="held", bufs=1) as held,
+        tc.tile_pool(name="work", bufs=2) as work,
+        tc.psum_pool(name="psum", bufs=S // BANK) as psum,
+    ):
+        offsets = lists.tile([128, D * V // 16], U16, name="offsets")
+        weights = held.tile([128, HALVES, R], BF16, name="weights")
+        centres = held.tile([R, V], F32, name="centres")
+        tab = held.tile([R, S], F32, name="tab")
+
+        nc.sync.dma_start(weights[:], wt.rearrange("(h p) r -> p h r", p=128))
+        z_halves = z.rearrange("(h p) s -> p h s", p=128)
+        chunks = []
+        for c in range(S // BANK):
+            chunk = held.tile([128, HALVES, BANK], BF16, name=f"z{c}")
+            nc.sync.dma_start(chunk[:], z_halves[:, :, c * BANK : (c + 1) * BANK])
+            chunks.append(chunk)
+        nc.sync.dma_start(offsets[:], offs)
+        nc.sync.dma_start(centres[:], ctr)
+
+        for c, chunk in enumerate(chunks):
+            product = psum.tile([R, BANK], F32, name="product")
+            for h in range(HALVES):
+                nc.tensor.matmul(product[:], weights[:, h, :], chunk[:, h, :], start=h == 0, stop=h == HALVES - 1)
+            nc.scalar.copy(tab[:, c * BANK : (c + 1) * BANK], product[:])
+
+        for j in range(0, V, PIECE):
+            centre = centres[:, j : j + PIECE]
+            differences = []
+            for d in range(D):
+                a = (V * d + j) // 16
+                difference = work.tile([R, PIECE], F32, name=f"difference{d}")
+                nc.vector.tensor_tensor(difference[:], tab[:].indirect(offsets[:, a : a + PIECE // 16]), centre, SUB)
+                differences.append(difference)
+            first = work.tile([R, PIECE], F32, name="first")
+            nc.scalar.activation(first[:], differences[0][:], RELU)
+            x = work.tile([R, PIECE], F32, name="x")
+            nc.vector.scalar_tensor_tensor(x[:], differences[1][:], 0.0, first[:], MAX, ADD)
+            nc.sync.dma_start(out[:, j : j + PIECE], x[:])

@@ -7,6 +7,7 @@ RELU = mybir.ActivationFunctionType.Relu
 R, K, S, D, V = 128, 256, 2048, 2, 1024
 HALVES = K // 128
 BANK = 512
+WARM = 4
 PIECE = 512
 FLOPS = 2 * R * K * S + 3 * D * R * V
 
@@ -18,6 +19,7 @@ def tile_lookup_pjedge_out_kernel(tc, z, wt, ctr, offs, out):
         tc.tile_pool(name="held", bufs=1) as held,
         tc.tile_pool(name="work", bufs=2) as work,
         tc.psum_pool(name="psum", bufs=S // BANK) as psum,
+        tc.psum_pool(name="warm", bufs=1) as warm,
     ):
         offsets = lists.tile([128, D * V // 16], U16, name="offsets")
         weights = held.tile([128, HALVES, R], BF16, name="weights")
@@ -33,6 +35,12 @@ def tile_lookup_pjedge_out_kernel(tc, z, wt, ctr, offs, out):
             chunks.append(chunk)
         nc.sync.dma_start(offsets[:], offs)
         nc.sync.dma_start(centres[:], ctr)
+
+        zeros = held.tile([128, BANK], BF16, name="zeros")
+        nc.vector.memset(zeros[:], 0.0)
+        idle = warm.tile([R, BANK], F32, name="idle")
+        for w in range(WARM):
+            nc.tensor.matmul(idle[:], zeros[:, :R], zeros[:], start=True, stop=True)
 
         for c, chunk in enumerate(chunks):
             product = psum.tile([R, BANK], F32, name="product")

@@ -6,9 +6,10 @@ RELU = mybir.ActivationFunctionType.Relu
 
 R, K, S, D, V = 128, 256, 2048, 2, 1024
 HALVES = K // 128
-BANK = 512
-WARM = 4
-PIECE = 512
+LOAD = 512
+PART = 256
+WARM = 16
+STORE = 512
 FLOPS = 2 * R * K * S + 3 * D * R * V
 
 
@@ -17,47 +18,54 @@ def tile_lookup_pjedge_out_kernel(tc, z, wt, ctr, offs, out):
     with (
         tc.tile_pool(name="lists", bufs=1) as lists,
         tc.tile_pool(name="held", bufs=1) as held,
-        tc.tile_pool(name="work", bufs=2) as work,
-        tc.psum_pool(name="psum", bufs=S // BANK) as psum,
+        tc.psum_pool(name="psum", bufs=6) as psum,
         tc.psum_pool(name="warm", bufs=1) as warm,
     ):
         offsets = lists.tile([128, D * V // 16], U16, name="offsets")
         weights = held.tile([128, HALVES, R], BF16, name="weights")
-        centres = held.tile([R, V], F32, name="centres")
         tab = held.tile([R, S], F32, name="tab")
 
-        nc.sync.dma_start(weights[:], wt.rearrange("(h p) r -> p h r", p=128))
+        nc.scalar.dma_start(weights[:], wt.rearrange("(h p) r -> p h r", p=128))
         z_halves = z.rearrange("(h p) s -> p h s", p=128)
         chunks = []
-        for c in range(S // BANK):
-            chunk = held.tile([128, HALVES, BANK], BF16, name=f"z{c}")
-            nc.sync.dma_start(chunk[:], z_halves[:, :, c * BANK : (c + 1) * BANK])
+        for c in range(S // LOAD):
+            chunk = held.tile([128, HALVES, LOAD], BF16, name=f"z{c}")
+            nc.sync.dma_start(chunk[:], z_halves[:, :, c * LOAD : (c + 1) * LOAD])
             chunks.append(chunk)
         nc.sync.dma_start(offsets[:], offs)
+        centres = held.tile([R, V], F32, name="centres")
         nc.sync.dma_start(centres[:], ctr)
 
-        zeros = held.tile([128, BANK], BF16, name="zeros")
+        zeros = held.tile([128, R], BF16, name="zeros")
         nc.vector.memset(zeros[:], 0.0)
-        idle = warm.tile([R, BANK], F32, name="idle")
+        idle = warm.tile([R, R], F32, name="idle")
         for w in range(WARM):
-            nc.tensor.matmul(idle[:], zeros[:, :R], zeros[:], start=True, stop=True)
+            nc.tensor.matmul(idle[:], zeros[:], zeros[:], start=True, stop=True)
 
-        for c, chunk in enumerate(chunks):
-            product = psum.tile([R, BANK], F32, name="product")
+        for i in range(S // PART):
+            c, a = divmod(i * PART, LOAD)
+            product = psum.tile([R, PART], F32, name="product")
             for h in range(HALVES):
-                nc.tensor.matmul(product[:], weights[:, h, :], chunk[:, h, :], start=h == 0, stop=h == HALVES - 1)
-            nc.scalar.copy(tab[:, c * BANK : (c + 1) * BANK], product[:])
+                nc.tensor.matmul(
+                    product[:], weights[:, h, :], chunks[c][:, h, a : a + PART], start=h == 0, stop=h == HALVES - 1
+                )
+            columns = tab[:, i * PART : (i + 1) * PART]
+            if i % 2 == 0:
+                nc.scalar.copy(columns, product[:])
+            else:
+                nc.vector.tensor_copy(columns, product[:])
 
-        for j in range(0, V, PIECE):
-            centre = centres[:, j : j + PIECE]
-            differences = []
-            for d in range(D):
-                a = (V * d + j) // 16
-                difference = work.tile([R, PIECE], F32, name=f"difference{d}")
-                nc.vector.tensor_tensor(difference[:], tab[:].indirect(offsets[:, a : a + PIECE // 16]), centre, SUB)
-                differences.append(difference)
-            first = work.tile([R, PIECE], F32, name="first")
-            nc.scalar.activation(first[:], differences[0][:], RELU)
-            x = work.tile([R, PIECE], F32, name="x")
-            nc.vector.scalar_tensor_tensor(x[:], differences[1][:], 0.0, first[:], MAX, ADD)
-            nc.sync.dma_start(out[:, j : j + PIECE], x[:])
+        differences = []
+        for d in range(D):
+            difference = held.tile([R, V], F32, name=f"difference{d}")
+            picked = tab[:].indirect(offsets[:, d * V // 16 : (d + 1) * V // 16])
+            nc.vector.tensor_tensor(difference[:], picked, centres[:], SUB)
+            differences.append(difference)
+
+        first = held.tile([R, V], F32, name="first")
+        nc.scalar.activation(first[:], differences[0][:], RELU)
+        for j in range(0, V, STORE):
+            x = held.tile([R, STORE], F32, name=f"x{j}")
+            columns = slice(j, j + STORE)
+            nc.vector.scalar_tensor_tensor(x[:], differences[1][:, columns], 0.0, first[:, columns], MAX, ADD)
+            nc.sync.dma_start(out[:, columns], x[:])

@@ -9,7 +9,7 @@ HALVES = K // 128
 LOAD = 512
 PART = 256
 WARM = 16
-STORE = 512
+PIECE = 512
 FLOPS = 2 * R * K * S + 3 * D * R * V
 
 
@@ -33,8 +33,12 @@ def tile_lookup_pjedge_out_kernel(tc, z, wt, ctr, offs, out):
             nc.sync.dma_start(chunk[:], z_halves[:, :, c * LOAD : (c + 1) * LOAD])
             chunks.append(chunk)
         nc.sync.dma_start(offsets[:], offs)
-        centres = held.tile([R, V], F32, name="centres")
-        nc.sync.dma_start(centres[:], ctr)
+        pieces = [slice(j, j + PIECE) for j in range(0, V, PIECE)]
+        centres = []
+        for p, columns in enumerate(pieces):
+            centre = held.tile([R, PIECE], F32, name=f"centre{p}")
+            nc.sync.dma_start(centre[:], ctr[:, columns])
+            centres.append(centre)
 
         zeros = held.tile([128, R], BF16, name="zeros")
         nc.vector.memset(zeros[:], 0.0)
@@ -55,17 +59,17 @@ def tile_lookup_pjedge_out_kernel(tc, z, wt, ctr, offs, out):
             else:
                 nc.vector.tensor_copy(columns, product[:])
 
-        differences = []
+        differences = {}
         for d in range(D):
-            difference = held.tile([R, V], F32, name=f"difference{d}")
-            picked = tab[:].indirect(offsets[:, d * V // 16 : (d + 1) * V // 16])
-            nc.vector.tensor_tensor(difference[:], picked, centres[:], SUB)
-            differences.append(difference)
+            for p, columns in enumerate(pieces):
+                difference = held.tile([R, PIECE], F32, name=f"difference{d}_{p}")
+                entries = offsets[:, (V * d + columns.start) // 16 : (V * d + columns.stop) // 16]
+                nc.vector.tensor_tensor(difference[:], tab[:].indirect(entries), centres[p][:], SUB)
+                differences[d, p] = difference
 
-        first = held.tile([R, V], F32, name="first")
-        nc.scalar.activation(first[:], differences[0][:], RELU)
-        for j in range(0, V, STORE):
-            x = held.tile([R, STORE], F32, name=f"x{j}")
-            columns = slice(j, j + STORE)
-            nc.vector.scalar_tensor_tensor(x[:], differences[1][:, columns], 0.0, first[:, columns], MAX, ADD)
+        for p, columns in enumerate(pieces):
+            first = held.tile([R, PIECE], F32, name=f"first{p}")
+            nc.scalar.activation(first[:], differences[0, p][:], RELU)
+            x = held.tile([R, PIECE], F32, name=f"x{p}")
+            nc.vector.scalar_tensor_tensor(x[:], differences[1, p][:], 0.0, first[:], MAX, ADD)
             nc.sync.dma_start(out[:, columns], x[:])

@@ -6,10 +6,10 @@ RELU = mybir.ActivationFunctionType.Relu
 
 R, K, S, D, V = 128, 256, 2048, 2, 1024
 HALVES = K // 128
-LOAD = 512
+FIRST_LOAD, SECOND_LOAD = 1024, 512
 PART = 256
 WARM = 16
-PIECE = 512
+PIECE, STORE = 512, 256
 FLOPS = 2 * R * K * S + 3 * D * R * V
 
 
@@ -18,20 +18,19 @@ def tile_lookup_pjedge_out_kernel(tc, z, wt, ctr, offs, out):
     with (
         tc.tile_pool(name="lists", bufs=1) as lists,
         tc.tile_pool(name="held", bufs=1) as held,
-        tc.psum_pool(name="psum", bufs=6) as psum,
-        tc.psum_pool(name="warm", bufs=1) as warm,
+        tc.psum_pool(name="psum", bufs=1) as psum,
     ):
         offsets = lists.tile([128, D * V // 16], U16, name="offsets")
         weights = held.tile([128, HALVES, R], BF16, name="weights")
         tab = held.tile([R, S], F32, name="tab")
 
         nc.scalar.dma_start(weights[:], wt.rearrange("(h p) r -> p h r", p=128))
-        z_halves = z.rearrange("(h p) s -> p h s", p=128)
-        chunks = []
-        for c in range(S // LOAD):
-            chunk = held.tile([128, HALVES, LOAD], BF16, name=f"z{c}")
-            nc.sync.dma_start(chunk[:], z_halves[:, :, c * LOAD : (c + 1) * LOAD])
-            chunks.append(chunk)
+        z_parts = {}
+        for h, width in enumerate((FIRST_LOAD, SECOND_LOAD)):
+            for c in range(0, S, width):
+                part = held.tile([128, width], BF16, name=f"z{h}_{c}")
+                nc.sync.dma_start(part[:], z[128 * h : 128 * (h + 1), c : c + width])
+                z_parts[h, c] = part
         nc.sync.dma_start(offsets[:], offs)
         pieces = [slice(j, j + PIECE) for j in range(0, V, PIECE)]
         centres = []
@@ -40,24 +39,26 @@ def tile_lookup_pjedge_out_kernel(tc, z, wt, ctr, offs, out):
             nc.sync.dma_start(centre[:], ctr[:, columns])
             centres.append(centre)
 
+        sums = [psum.tile([R, PART], F32, name=f"sums{i}") for i in range(S // PART)]
+
         zeros = held.tile([128, R], BF16, name="zeros")
         nc.vector.memset(zeros[:], 0.0)
-        idle = warm.tile([R, R], F32, name="idle")
         for w in range(WARM):
-            nc.tensor.matmul(idle[:], zeros[:], zeros[:], start=True, stop=True)
+            nc.tensor.matmul(sums[0][:, :R], zeros[:], zeros[:], start=True, stop=True)
 
         for i in range(S // PART):
-            c, a = divmod(i * PART, LOAD)
-            product = psum.tile([R, PART], F32, name="product")
-            for h in range(HALVES):
-                nc.tensor.matmul(
-                    product[:], weights[:, h, :], chunks[c][:, h, a : a + PART], start=h == 0, stop=h == HALVES - 1
-                )
+            c = i * PART // FIRST_LOAD * FIRST_LOAD
+            moving = z_parts[0, c][:, i * PART - c : (i + 1) * PART - c]
+            nc.tensor.matmul(sums[i][:], weights[:, 0, :], moving, start=True, stop=False)
+        for i in range(S // PART):
+            c = i * PART // SECOND_LOAD * SECOND_LOAD
+            moving = z_parts[1, c][:, i * PART - c : (i + 1) * PART - c]
+            nc.tensor.matmul(sums[i][:], weights[:, 1, :], moving, start=False, stop=True)
             columns = tab[:, i * PART : (i + 1) * PART]
             if i % 2 == 0:
-                nc.scalar.copy(columns, product[:])
+                nc.scalar.copy(columns, sums[i][:])
             else:
-                nc.vector.tensor_copy(columns, product[:])
+                nc.vector.tensor_copy(columns, sums[i][:])
 
         differences = {}
         for d in range(D):
@@ -70,6 +71,8 @@ def tile_lookup_pjedge_out_kernel(tc, z, wt, ctr, offs, out):
         for p, columns in enumerate(pieces):
             first = held.tile([R, PIECE], F32, name=f"first{p}")
             nc.scalar.activation(first[:], differences[0, p][:], RELU)
-            x = held.tile([R, PIECE], F32, name=f"x{p}")
-            nc.vector.scalar_tensor_tensor(x[:], differences[1, p][:], 0.0, first[:], MAX, ADD)
-            nc.sync.dma_start(out[:, columns], x[:])
+            for a in range(0, PIECE, STORE):
+                part = slice(a, a + STORE)
+                x = held.tile([R, STORE], F32, name=f"x{p}_{a}")
+                nc.vector.scalar_tensor_tensor(x[:], differences[1, p][:, part], 0.0, first[:, part], MAX, ADD)
+                nc.sync.dma_start(out[:, columns.start + a : columns.start + a + STORE], x[:])

import concourse.mybir as mybir

F32, BF16, U16 = mybir.dt.float32, mybir.dt.bfloat16, mybir.dt.uint16
SUB, MAX, ADD = mybir.AluOpType.subtract, mybir.AluOpType.max, mybir.AluOpType.add
RELU = mybir.ActivationFunctionType.Relu

R, K, S, D, V = 128, 256, 2048, 2, 1024
HALVES = K // 128
FIRST_LOAD, SECOND_LOAD = 1024, 512
PART = 256
WARM = 16
PIECE, STORE = 512, 256
FLOPS = 2 * R * K * S + 3 * D * R * V


def tile_lookup_pjedge_out_kernel(tc, z, wt, ctr, offs, out):
    nc = tc.nc
    with (
        tc.tile_pool(name="lists", bufs=1) as lists,
        tc.tile_pool(name="held", bufs=1) as held,
        tc.psum_pool(name="psum", bufs=1) as psum,
    ):
        offsets = lists.tile([128, D * V // 16], U16, name="offsets")
        weights = held.tile([128, HALVES, R], BF16, name="weights")
        tab = held.tile([R, S], F32, name="tab")

        nc.scalar.dma_start(weights[:], wt.rearrange("(h p) r -> p h r", p=128))
        z_parts = {}
        for h, width in enumerate((FIRST_LOAD, SECOND_LOAD)):
            for c in range(0, S, width):
                part = held.tile([128, width], BF16, name=f"z{h}_{c}")
                nc.sync.dma_start(part[:], z[128 * h : 128 * (h + 1), c : c + width])
                z_parts[h, c] = part
        nc.sync.dma_start(offsets[:], offs)
        pieces = [slice(j, j + PIECE) for j in range(0, V, PIECE)]
        centres = []
        for p, columns in enumerate(pieces):
            centre = held.tile([R, PIECE], F32, name=f"centre{p}")
            nc.sync.dma_start(centre[:], ctr[:, columns])
            centres.append(centre)

        sums = [psum.tile([R, PART], F32, name=f"sums{i}") for i in range(S // PART)]

        zeros = held.tile([128, R], BF16, name="zeros")
        nc.vector.memset(zeros[:], 0.0)
        for w in range(WARM):
            nc.tensor.matmul(sums[0][:, :R], zeros[:], zeros[:], start=True, stop=True)

        for i in range(S // PART):
            c = i * PART // FIRST_LOAD * FIRST_LOAD
            moving = z_parts[0, c][:, i * PART - c : (i + 1) * PART - c]
            nc.tensor.matmul(sums[i][:], weights[:, 0, :], moving, start=True, stop=False)
        for i in range(S // PART):
            c = i * PART // SECOND_LOAD * SECOND_LOAD
            moving = z_parts[1, c][:, i * PART - c : (i + 1) * PART - c]
            nc.tensor.matmul(sums[i][:], weights[:, 1, :], moving, start=False, stop=True)
            columns = tab[:, i * PART : (i + 1) * PART]
            if i % 2 == 0:
                nc.scalar.copy(columns, sums[i][:])
            else:
                nc.vector.tensor_copy(columns, sums[i][:])

        differences = {}
        for d in range(D):
            for p, columns in enumerate(pieces):
                difference = held.tile([R, PIECE], F32, name=f"difference{d}_{p}")
                entries = offsets[:, (V * d + columns.start) // 16 : (V * d + columns.stop) // 16]
                nc.vector.tensor_tensor(difference[:], tab[:].indirect(entries), centres[p][:], SUB)
                differences[d, p] = difference

        for p, columns in enumerate(pieces):
            first = held.tile([R, PIECE], F32, name=f"first{p}")
            nc.scalar.activation(first[:], differences[0, p][:], RELU)
            for a in range(0, PIECE, STORE):
                part = slice(a, a + STORE)
                x = held.tile([R, STORE], F32, name=f"x{p}_{a}")
                nc.vector.scalar_tensor_tensor(x[:], differences[1, p][:, part], 0.0, first[:, part], MAX, ADD)
                nc.sync.dma_start(out[:, columns.start + a : columns.start + a + STORE], x[:])
